import numpy as np
import ml_dtypes


def mxq(x, axis, fmt="e4m3"):
    dtype, down = {"e4m3": (ml_dtypes.float8_e4m3fn, 7), "e5m2": (ml_dtypes.float8_e5m2, 14)}[fmt]
    v = np.moveaxis(np.asarray(x, np.float32).astype(ml_dtypes.bfloat16).astype(np.float64), axis, -1)
    blocks = v.reshape(v.shape[:-1] + (-1, 32))
    amax = np.abs(blocks).max(-1, keepdims=True)
    byte = np.maximum(np.where(amax > 0, np.frexp(amax)[1] - 1 + 127, 0) - down, 1)
    scale = np.exp2(byte - 127.0)
    codes = (blocks / scale).astype(np.float32).astype(dtype).astype(np.float64)
    return np.moveaxis((codes * scale).reshape(v.shape), -1, axis)


WIDE = False


def mx_kscale(k):
    if not WIDE:
        return np.ones(k)
    levels = np.array([30, -30])
    if k % 512:
        return np.exp2(np.random.permutation(np.resize(levels, k // 32))).repeat(32)
    a = np.empty((k // 512, 16))
    for p in range(k // 512):
        a[p, :8] = np.random.permutation(np.resize(levels, 8))
        for g in range(8):
            far = levels[np.abs(levels - a[p, g]) >= 10]
            a[p, g + 8] = far[np.random.randint(len(far))]
    return np.exp2(a.ravel()).repeat(32)


def f64(x):
    return np.asarray(x).astype(np.float64)


def striped(idx):
    return np.tile(np.asarray(idx).reshape(-1, 16).T, (8, 1)).astype(np.uint16)


def unstriped(offs):
    return offs[:16].T.reshape(-1).astype(np.int64)


E2M1 = np.array([0.0, 0.5, 1.0, 1.5, 2.0, 3.0, 4.0, 6.0, -0.0, -0.5, -1.0, -1.5, -2.0, -3.0, -4.0, -6.0])


def pack_weight(w, fmt):
    k, n = w.shape
    w = f64(np.asarray(w, np.float32).astype(ml_dtypes.bfloat16)).reshape(k // 32, 32, n)
    amax = np.abs(w).max(1)
    if fmt in ("e4m3", "e5m2"):
        byte = np.frexp(amax)[1] - 1 + 127 - (7 if fmt == "e4m3" else 14)
    else:
        mant, ex = np.frexp(amax / 6.0)
        byte = np.where(mant > 0.5, ex, ex - 1) + 127
    byte = np.clip(np.where(amax > 0, byte, 1), 1, 254)
    scaled = (w * np.exp2(127.0 - byte)[:, None, :]).reshape(k, n).astype(np.float32)
    by_word = np.ascontiguousarray(scaled.reshape(k // 512, 128, 4, n).transpose(0, 1, 3, 2))
    if fmt in ("e4m3", "e5m2"):
        words = by_word.astype(ml_dtypes.float8_e4m3fn if fmt == "e4m3" else ml_dtypes.float8_e5m2).view(np.uint8)
    else:
        c = by_word.astype(ml_dtypes.float4_e2m1fn).view(np.uint8) & 0xF
        words = (c[..., 0::2] | (c[..., 1::2] << 4)).reshape(k // 512, 128, 2 * n)
    return np.ascontiguousarray(words), np.ascontiguousarray(byte.astype(np.uint8).reshape(k // 512, 16, n))


def unpack_weight(words, scales, fmt):
    g, _, n = scales.shape
    words = np.ascontiguousarray(words).reshape(g, 128, n, -1)
    if fmt in ("e4m3", "e5m2"):
        vals = words.view(ml_dtypes.float8_e4m3fn if fmt == "e4m3" else ml_dtypes.float8_e5m2).astype(np.float64)
    else:
        nib = np.empty((g, 128, n, 4), np.uint8)
        nib[..., 0::2] = words & 0xF
        nib[..., 1::2] = words >> 4
        vals = E2M1[nib]
    vals = vals * np.repeat(np.exp2(scales.astype(np.float64) - 127.0), 8, axis=1)[..., None]
    return vals.transpose(0, 1, 3, 2).reshape(g * 512, n)


def sigmoid(v):
    return 1.0 / (1.0 + np.exp(-v))


K, T, J, R, O, N, L, E = 512, 2048, 256, 512, 128, 256, 512, 512


def setup_inputs():
    n = np.random.standard_normal
    idx = np.random.permutation(T)[:J]
    idx2 = np.random.permutation(T)[:J]
    idx3 = np.random.permutation(J)[:O]
    idx4 = np.random.permutation(J)[:O]
    idx5 = np.random.permutation(E)[:O]
    fk = mx_kscale(K)
    fr = mx_kscale(R)
    fl = mx_kscale(L)
    xtp = pack_weight(n((K, T)) / fk[:, None], "e2m1")
    wp = pack_weight(n((K, R)) * 1 / np.sqrt(K) * fk[:, None], "e4m3")
    w2p = pack_weight(n((K, R)) * 1 / np.sqrt(K) * fk[:, None] * fr, "e5m2")
    wbp = pack_weight(n((R, N)) * 1 / np.sqrt(R) / fr[:, None], "e2m1")
    sxp = pack_weight(n((L, O)) / fl[:, None], "e4m3")
    wsp = pack_weight(n((L, N)) * 1 / np.sqrt(L) * fl[:, None], "e4m3")
    return {
        "xt_words": xtp[0],
        "xt_scales": xtp[1],
        "w_words": wp[0],
        "w_scales": wp[1],
        "w2_words": w2p[0],
        "w2_scales": w2p[1],
        "sg": (np.random.uniform(0.6, 1.6, (R, 1))).astype(np.float32),
        "wb_words": wbp[0],
        "wb_scales": wbp[1],
        "sx_words": sxp[0],
        "sx_scales": sxp[1],
        "ws_words": wsp[0],
        "ws_scales": wsp[1],
        "tz": (n((N, E))).astype(np.float32),
        "so": (np.random.uniform(0.6, 1.6, (N, 1))).astype(np.float32),
        "bo": (np.random.uniform(-1.0, 1.0, (N, 1))).astype(np.float32),
        "offs": striped(idx),
        "offs2": striped(idx2),
        "offs3": striped(idx3),
        "offs4": striped(idx4),
        "offs5": striped(idx5),
    }


def reference(xt_words, xt_scales, w_words, w_scales, w2_words, w2_scales, sg, wb_words, wb_scales, sx_words, sx_scales, ws_words, ws_scales, tz, so, bo, offs, offs2, offs3, offs4, offs5):
    idx = unstriped(offs)
    idx2 = unstriped(offs2)
    idx3 = unstriped(offs3)
    idx4 = unstriped(offs4)
    idx5 = unstriped(offs5)
    xtu = unpack_weight(xt_words, xt_scales, "e2m1")
    wu = unpack_weight(w_words, w_scales, "e4m3")
    w2u = unpack_weight(w2_words, w2_scales, "e5m2")
    wbu = unpack_weight(wb_words, wb_scales, "e2m1")
    sxu = unpack_weight(sx_words, sx_scales, "e4m3")
    wsu = unpack_weight(ws_words, ws_scales, "e4m3")
    xtidxg = xtu[:, idx]
    a = wu.T @ xtidxg
    xtidx2g = xtu[:, idx2]
    b = w2u.T @ xtidx2g
    hid = np.maximum(b[:, idx3], b[:, idx4]) * sigmoid(a[:, idx4] * f64(sg))
    hidq = mxq(hid, 0, "e5m2")
    p = wbu.T @ hidq + wsu.T @ sxu
    y = p * sigmoid(f64(tz)[:, idx5] * f64(so) + f64(bo))
    return y

@@ -1,0 +1,180 @@
+from contextlib import ExitStack
+
+import concourse.mybir as mybir
+
+K, T, J, R, O, N, L, E = 512, 2048, 256, 512, 128, 256, 512, 512
+FLOPS = 2 * (2 * K * R * J + R * N * O + L * N * O)
+
+F32 = mybir.dt.float32
+BF16 = mybir.dt.bfloat16
+I32 = mybir.dt.int32
+U32 = mybir.dt.uint32
+U16 = mybir.dt.uint16
+U8 = mybir.dt.uint8
+E4M3 = mybir.dt.float8_e4m3fn_x4
+E5M2 = mybir.dt.float8_e5m2_x4
+E2M1 = mybir.dt.float4_e2m1fn_x4
+ACT = mybir.ActivationFunctionType
+ALU = mybir.AluOpType
+
+P = 128
+PACK = 4
+QUADS = 4
+
+
+def load_scale_rows(queue, plane, scales):
+    rows = scales[0].bitcast(I32)
+    for q in range(QUADS):
+        queue.dma_start(out=plane[32 * q : 32 * q + 4, :].bitcast(I32), in_=rows[4 * q : 4 * q + 4, :])
+
+
+def fp8_words(words):
+    return words[0].rearrange("p c t -> p (c t)").bitcast(I32)
+
+
+def tile_list_ahead_agree_skip_finalgate_kernel(
+    tc, xt_words, xt_scales, w_words, w_scales, w2_words, w2_scales, sg, wb_words, wb_scales,
+    sx_words, sx_scales, ws_words, ws_scales, tz, so, bo, offs, offs2, offs3, offs4, offs5, out,
+):
+    nc = tc.nc
+    with ExitStack() as ctx:
+        sb = ctx.enter_context(tc.tile_pool(name="sb", bufs=1))
+        ps = ctx.enter_context(tc.psum_pool(name="ps", bufs=1))
+
+        def tile(name, shape, dtype):
+            return sb.tile(shape, dtype, name=name, align_bytes=64)
+
+        list1 = tile("list1", [P, J // 16], U16)
+        list2 = tile("list2", [P, J // 16], U16)
+        list3 = tile("list3", [P, O // 16], U16)
+        list4 = tile("list4", [P, O // 16], U16)
+        list5 = tile("list5", [P, O // 16], U16)
+        xt_w = tile("xt_w", [P, T], U16)
+        xt_s = tile("xt_s", [P, T], U8)
+        w1_raw = tile("w1_raw", [P, R], U32)
+        w2_raw = tile("w2_raw", [P, R], U32)
+        planes = tile("planes", [P, 2 * R + 2 * N + O], U8)
+        w2_sraw = planes[:, 0:R]
+        w1_sraw = planes[:, R : 2 * R]
+        ws_s = planes[:, 2 * R : 2 * R + N]
+        wb_s = planes[:, 2 * R + N : 2 * R + 2 * N]
+        sx_s = planes[:, 2 * R + 2 * N :]
+
+        nc.vector.memset(xt_s[:].bitcast(I32), 0)
+        nc.vector.memset(planes[:].bitcast(I32), 0)
+        nc.sync.dma_start(out=xt_w[:].bitcast(I32), in_=xt_words[0].bitcast(I32))
+        nc.sync.dma_start(out=list2[:], in_=offs2)
+        load_scale_rows(nc.scalar, xt_s, xt_scales)
+        nc.sync.dma_start(out=list1[:], in_=offs)
+        nc.sync.dma_start(out=w2_raw[:].bitcast(I32), in_=fp8_words(w2_words))
+        load_scale_rows(nc.sync, w2_sraw, w2_scales)
+        nc.sync.dma_start(out=w1_raw[:].bitcast(I32), in_=fp8_words(w_words))
+        load_scale_rows(nc.sync, w1_sraw, w_scales)
+        nc.sync.dma_start(out=list3[:], in_=offs3)
+        nc.sync.dma_start(out=list4[:], in_=offs4)
+        slope = tile("slope", [P, PACK], F32)
+        nc.sync.dma_start(out=slope[:], in_=sg.rearrange("(p t) o -> p (t o)", t=PACK))
+
+        halves = N // P
+        gate_table = [tile("gate_table%d" % h, [P, E], F32) for h in range(halves)]
+        gate_slope = tile("gate_slope", [P, halves], F32)
+        gate_offset = tile("gate_offset", [P, halves], F32)
+        ws_w = tile("ws_w", [P, N], U32)
+        sx_w = tile("sx_w", [P, O], U32)
+        wb_w = tile("wb_w", [P, 2 * N], U8)
+        nc.sync.dma_start(out=ws_w[:].bitcast(I32), in_=fp8_words(ws_words))
+        load_scale_rows(nc.sync, ws_s, ws_scales)
+        nc.sync.dma_start(out=sx_w[:].bitcast(I32), in_=fp8_words(sx_words))
+        load_scale_rows(nc.sync, sx_s, sx_scales)
+        nc.sync.dma_start(out=wb_w[:].bitcast(I32), in_=wb_words[0].bitcast(I32))
+        load_scale_rows(nc.sync, wb_s, wb_scales)
+        nc.sync.dma_start(out=list5[:], in_=offs5)
+        with nc.allow_non_contiguous_dma(reason="one value for each partition"):
+            nc.sync.dma_start(out=gate_slope[:], in_=so.rearrange("(h p) o -> p (h o)", p=P))
+            nc.sync.dma_start(out=gate_offset[:], in_=bo.rearrange("(h p) o -> p (h o)", p=P))
+        for h in range(halves):
+            nc.sync.dma_start(out=gate_table[h][:], in_=tz[h * P : (h + 1) * P, :])
+
+        def first_stage(name, offsets, raw, sraw, fmt, banks):
+            picked_s = tile(name + "_picked_s", [P, J], U8)
+            picked_w = tile(name + "_picked_w", [P, J], U16)
+            dealt_w = tile(name + "_dealt_w", [P, R], U32)
+            dealt_s = tile(name + "_dealt_s", [P, R], U8)
+            nc.vector.tensor_copy(out=picked_s[:], in_=xt_s[:].indirect(offsets[:]))
+            nc.vector.tensor_copy(out=picked_w[:], in_=xt_w[:].indirect(offsets[:]))
+            nc.scalar.copy(
+                out=dealt_w[:].rearrange("p (t m) -> p m t", t=PACK),
+                in_=raw[:].rearrange("p (m t) -> p m t", t=PACK),
+            )
+            nc.vector.tensor_copy(
+                out=dealt_s[:].rearrange("p (t m) -> p m t", t=PACK),
+                in_=sraw.rearrange("p (m t) -> p m t", t=PACK),
+            )
+            for t in range(PACK):
+                cols = slice(t * P, (t + 1) * P)
+                nc.tensor.matmul_mx(
+                    out=banks[t],
+                    lhsT=dealt_w[:, cols].bitcast(fmt),
+                    lhsT_scale=dealt_s[:, cols],
+                    rhs=picked_w[:].bitcast(E2M1),
+                    rhs_scale=picked_s[:],
+                    start=True,
+                    stop=True,
+                )
+
+        b_ps = [ps.tile([P, J], F32, name="b_ps%d" % t) for t in range(PACK)]
+        a_ps = [ps.tile([P, 2, J], F32, name="a_ps%d" % u) for u in range(PACK // 2)]
+        first_stage("b", list2, w2_raw, w2_sraw, E5M2, [b_ps[t][:] for t in range(PACK)])
+        b_sb = [tile("b_sb%d" % t, [P, J], F32) for t in range(PACK)]
+        for t in range(PACK):
+            nc.scalar.copy(out=b_sb[t][:], in_=b_ps[t][:])
+        first_stage("a", list1, w1_raw, w1_sraw, E4M3, [a_ps[t // 2][:, t % 2, :] for t in range(PACK)])
+
+        b3 = tile("b3", [P, PACK, O], F32)
+        b4 = tile("b4", [P, PACK, O], F32)
+        larger = tile("larger", [P, PACK, O], F32)
+        gate = tile("gate", [P, PACK, O], F32)
+        a_sb = [tile("a_sb%d" % t, [P, J], F32) for t in range(PACK)]
+        for t in range(PACK):
+            nc.vector.tensor_copy(out=b3[:, t, :], in_=b_sb[t][:].indirect(list3[:]))
+            nc.vector.tensor_copy(out=b4[:, t, :], in_=b_sb[t][:].indirect(list4[:]))
+            nc.scalar.copy(out=a_sb[t][:], in_=a_ps[t // 2][:, t % 2, :])
+            nc.scalar.activation(
+                out=gate[:, t, :], in_=a_sb[t][:].indirect(list4[:]), func=ACT.Sigmoid, scale=slope[:, t : t + 1]
+            )
+        nc.vector.tensor_tensor(out=larger[:], in0=b3[:], in1=b4[:], op=ALU.max)
+        hid = tile("hid", [P, O, PACK], BF16)
+        nc.vector.tensor_tensor(
+            out=hid[:].rearrange("p (c i) t -> p c t i", i=4),
+            in0=larger[:].rearrange("p t (c i) -> p c t i", i=4),
+            in1=gate[:].rearrange("p t (c i) -> p c t i", i=4),
+            op=ALU.mult,
+        )
+        hid_w = tile("hid_w", [P, O], U32)
+        hid_s = tile("hid_s", [P, O], U8)
+        nc.vector.quantize_mx(
+            out=hid_w[:].bitcast(E5M2), scales=hid_s[:], in_=hid[:].rearrange("p o t -> p (o t)")
+        )
+
+        stores = [nc.sync, nc.scalar]
+        p_ps = [ps.tile([P, O], F32, name="p_ps%d" % h) for h in range(halves)]
+        for h in range(halves):
+            cols = slice(h * P, (h + 1) * P)
+            nc.tensor.matmul_mx(
+                out=p_ps[h][:], lhsT=ws_w[:, cols].bitcast(E4M3), lhsT_scale=ws_s[:, cols],
+                rhs=sx_w[:].bitcast(E4M3), rhs_scale=sx_s, start=True, stop=False,
+            )
+        for h in range(halves):
+            cols = slice(h * P, (h + 1) * P)
+            last_gate = tile("last_gate%d" % h, [P, O], F32)
+            nc.scalar.activation(
+                out=last_gate[:], in_=gate_table[h][:].indirect(list5[:]), func=ACT.Sigmoid,
+                bias=gate_offset[:, h : h + 1], scale=gate_slope[:, h : h + 1],
+            )
+            nc.tensor.matmul_mx(
+                out=p_ps[h][:], lhsT=wb_w[:, 2 * h * P : 2 * (h + 1) * P].bitcast(E2M1), lhsT_scale=wb_s[:, cols],
+                rhs=hid_w[:].bitcast(E5M2), rhs_scale=hid_s[:], start=False, stop=True,
+            )
+            result = tile("result%d" % h, [P, O], F32)
+            nc.vector.tensor_tensor(out=result[:], in0=p_ps[h][:], in1=last_gate[:], op=ALU.mult)
+            stores[h].dma_start(out=out[cols, :], in_=result[:])

@@ -53,22 +53,31 @@ def tile_list_ahead_agree_skip_finalgate_kernel(
         xt_s = tile("xt_s", [P, T], U8)
         w1_raw = tile("w1_raw", [P, R], U32)
         w2_raw = tile("w2_raw", [P, R], U32)
-        planes = tile("planes", [P, 2 * R + 2 * N + O], U8)
-        w2_sraw = planes[:, 0:R]
-        w1_sraw = planes[:, R : 2 * R]
-        ws_s = planes[:, 2 * R : 2 * R + N]
-        wb_s = planes[:, 2 * R + N : 2 * R + 2 * N]
-        sx_s = planes[:, 2 * R + 2 * N :]
+        w2_sraw = tile("w2_sraw", [P, R], U8)
+        late = tile("late", [P, R + 2 * N + O], U8)
+        w1_sraw = late[:, 0:R]
+        ws_s = late[:, R : R + N]
+        wb_s = late[:, R + N : R + 2 * N]
+        sx_s = late[:, R + 2 * N :]
+
+        def w2_rows(q):
+            four = w2_scales[0].bitcast(I32)[4 * q : 4 * q + 4, :]
+            nc.sync.dma_start(
+                out=w2_sraw[32 * q : 32 * (q + 1), :].bitcast(I32),
+                in_=four.unsqueeze(0).broadcast_to([8, 4, R // 4]),
+            )
 
         nc.vector.memset(xt_s[:].bitcast(I32), 0)
-        nc.vector.memset(planes[:].bitcast(I32), 0)
-        nc.sync.dma_start(out=xt_w[:].bitcast(I32), in_=xt_words[0].bitcast(I32))
+        nc.vector.memset(late[:].bitcast(I32), 0)
+        nc.gpsimd.dma_start(out=w2_raw[:].bitcast(I32), in_=fp8_words(w2_words))
+        nc.gpsimd.dma_start(out=w1_raw[:].bitcast(I32), in_=fp8_words(w_words))
         nc.sync.dma_start(out=list2[:], in_=offs2)
+        w2_rows(0)
+        nc.sync.dma_start(out=xt_w[:].bitcast(I32), in_=xt_words[0].bitcast(I32))
         load_scale_rows(nc.scalar, xt_s, xt_scales)
+        for q in range(1, QUADS):
+            w2_rows(q)
         nc.sync.dma_start(out=list1[:], in_=offs)
-        nc.sync.dma_start(out=w2_raw[:].bitcast(I32), in_=fp8_words(w2_words))
-        load_scale_rows(nc.sync, w2_sraw, w2_scales)
-        nc.sync.dma_start(out=w1_raw[:].bitcast(I32), in_=fp8_words(w_words))
         load_scale_rows(nc.sync, w1_sraw, w_scales)
         nc.sync.dma_start(out=list3[:], in_=offs3)
         nc.sync.dma_start(out=list4[:], in_=offs4)
@@ -82,16 +91,16 @@ def tile_list_ahead_agree_skip_finalgate_kernel(
         ws_w = tile("ws_w", [P, N], U32)
         sx_w = tile("sx_w", [P, O], U32)
         wb_w = tile("wb_w", [P, 2 * N], U8)
-        nc.sync.dma_start(out=ws_w[:].bitcast(I32), in_=fp8_words(ws_words))
-        load_scale_rows(nc.sync, ws_s, ws_scales)
-        nc.sync.dma_start(out=sx_w[:].bitcast(I32), in_=fp8_words(sx_words))
-        load_scale_rows(nc.sync, sx_s, sx_scales)
-        nc.sync.dma_start(out=wb_w[:].bitcast(I32), in_=wb_words[0].bitcast(I32))
-        load_scale_rows(nc.sync, wb_s, wb_scales)
+        nc.gpsimd.dma_start(out=ws_w[:].bitcast(I32), in_=fp8_words(ws_words))
+        nc.gpsimd.dma_start(out=sx_w[:].bitcast(I32), in_=fp8_words(sx_words))
+        nc.gpsimd.dma_start(out=wb_w[:].bitcast(I32), in_=wb_words[0].bitcast(I32))
         nc.sync.dma_start(out=list5[:], in_=offs5)
         with nc.allow_non_contiguous_dma(reason="one value for each partition"):
             nc.sync.dma_start(out=gate_slope[:], in_=so.rearrange("(h p) o -> p (h o)", p=P))
             nc.sync.dma_start(out=gate_offset[:], in_=bo.rearrange("(h p) o -> p (h o)", p=P))
+        load_scale_rows(nc.sync, ws_s, ws_scales)
+        load_scale_rows(nc.sync, sx_s, sx_scales)
+        load_scale_rows(nc.sync, wb_s, wb_scales)
         for h in range(halves):
             nc.sync.dma_start(out=gate_table[h][:], in_=tz[h * P : (h + 1) * P, :])
 
@@ -122,13 +131,13 @@ def tile_list_ahead_agree_skip_finalgate_kernel(
                     stop=True,
                 )
 
-        b_ps = [ps.tile([P, J], F32, name="b_ps%d" % t) for t in range(PACK)]
-        a_ps = [ps.tile([P, 2, J], F32, name="a_ps%d" % u) for u in range(PACK // 2)]
-        first_stage("b", list2, w2_raw, w2_sraw, E5M2, [b_ps[t][:] for t in range(PACK)])
+        b_ps = [ps.tile([P, J], F32, name="b_ps%d" % t, tag="b_ps%d" % t) for t in range(PACK)]
+        a_ps = [ps.tile([P, J], F32, name="a_ps%d" % t) for t in range(PACK)]
+        first_stage("b", list2, w2_raw, w2_sraw[:], E5M2, [b_ps[t][:] for t in range(PACK)])
         b_sb = [tile("b_sb%d" % t, [P, J], F32) for t in range(PACK)]
         for t in range(PACK):
             nc.scalar.copy(out=b_sb[t][:], in_=b_ps[t][:])
-        first_stage("a", list1, w1_raw, w1_sraw, E4M3, [a_ps[t // 2][:, t % 2, :] for t in range(PACK)])
+        first_stage("a", list1, w1_raw, w1_sraw, E4M3, [a_ps[t][:] for t in range(PACK)])
 
         b3 = tile("b3", [P, PACK, O], F32)
         b4 = tile("b4", [P, PACK, O], F32)
@@ -136,9 +145,15 @@ def tile_list_ahead_agree_skip_finalgate_kernel(
         gate = tile("gate", [P, PACK, O], F32)
         a_sb = [tile("a_sb%d" % t, [P, J], F32) for t in range(PACK)]
         for t in range(PACK):
-            nc.vector.tensor_copy(out=b3[:, t, :], in_=b_sb[t][:].indirect(list3[:]))
+            if t < 2:
+                nc.scalar.activation(out=b3[:, t, :], in_=b_sb[t][:].indirect(list3[:]), func=ACT.Copy)
+            else:
+                nc.vector.tensor_copy(out=b3[:, t, :], in_=b_sb[t][:].indirect(list3[:]))
             nc.vector.tensor_copy(out=b4[:, t, :], in_=b_sb[t][:].indirect(list4[:]))
-            nc.scalar.copy(out=a_sb[t][:], in_=a_ps[t // 2][:, t % 2, :])
+            if t == 1:
+                nc.vector.tensor_copy(out=a_sb[t][:], in_=a_ps[t][:])
+            else:
+                nc.scalar.copy(out=a_sb[t][:], in_=a_ps[t][:])
             nc.scalar.activation(
                 out=gate[:, t, :], in_=a_sb[t][:].indirect(list4[:]), func=ACT.Sigmoid, scale=slope[:, t : t + 1]
             )
@@ -157,7 +172,7 @@ def tile_list_ahead_agree_skip_finalgate_kernel(
         )
 
         stores = [nc.sync, nc.scalar]
-        p_ps = [ps.tile([P, O], F32, name="p_ps%d" % h) for h in range(halves)]
+        p_ps = [ps.tile([P, O], F32, name="p_ps%d" % h, tag="b_ps%d" % h) for h in range(halves)]
         for h in range(halves):
             cols = slice(h * P, (h + 1) * P)
             nc.tensor.matmul_mx(

@@ -75,6 +75,10 @@ def tile_list_ahead_agree_skip_finalgate_kernel(
         w2_rows(0)
         nc.sync.dma_start(out=xt_w[:].bitcast(I32), in_=xt_words[0].bitcast(I32))
         load_scale_rows(nc.scalar, xt_s, xt_scales)
+        warm_in = tile("warm_in", [P, 1], F32)
+        warm_out = tile("warm_out", [P, 1], F32)
+        nc.vector.memset(warm_in[:], 0.0)
+        nc.scalar.activation(out=warm_out[:], in_=warm_in[:], func=ACT.Sigmoid)
         for q in range(1, QUADS):
             w2_rows(q)
         nc.sync.dma_start(out=list1[:], in_=offs)

from contextlib import ExitStack

import concourse.mybir as mybir

K, T, J, R, O, N, L, E = 512, 2048, 256, 512, 128, 256, 512, 512
FLOPS = 2 * (2 * K * R * J + R * N * O + L * N * O)

F32 = mybir.dt.float32
BF16 = mybir.dt.bfloat16
I32 = mybir.dt.int32
U32 = mybir.dt.uint32
U16 = mybir.dt.uint16
U8 = mybir.dt.uint8
E4M3 = mybir.dt.float8_e4m3fn_x4
E5M2 = mybir.dt.float8_e5m2_x4
E2M1 = mybir.dt.float4_e2m1fn_x4
ACT = mybir.ActivationFunctionType
ALU = mybir.AluOpType

P = 128
PACK = 4
QUADS = 4


def load_scale_rows(queue, plane, scales):
    rows = scales[0].bitcast(I32)
    for q in range(QUADS):
        queue.dma_start(out=plane[32 * q : 32 * q + 4, :].bitcast(I32), in_=rows[4 * q : 4 * q + 4, :])


def fp8_words(words):
    return words[0].rearrange("p c t -> p (c t)").bitcast(I32)


def tile_list_ahead_agree_skip_finalgate_kernel(
    tc, xt_words, xt_scales, w_words, w_scales, w2_words, w2_scales, sg, wb_words, wb_scales,
    sx_words, sx_scales, ws_words, ws_scales, tz, so, bo, offs, offs2, offs3, offs4, offs5, out,
):
    nc = tc.nc
    with ExitStack() as ctx:
        sb = ctx.enter_context(tc.tile_pool(name="sb", bufs=1))
        ps = ctx.enter_context(tc.psum_pool(name="ps", bufs=1))

        def tile(name, shape, dtype):
            return sb.tile(shape, dtype, name=name, align_bytes=64)

        list1 = tile("list1", [P, J // 16], U16)
        list2 = tile("list2", [P, J // 16], U16)
        list3 = tile("list3", [P, O // 16], U16)
        list4 = tile("list4", [P, O // 16], U16)
        list5 = tile("list5", [P, O // 16], U16)
        xt_w = tile("xt_w", [P, T], U16)
        xt_s = tile("xt_s", [P, T], U8)
        w1_raw = tile("w1_raw", [P, R], U32)
        w2_raw = tile("w2_raw", [P, R], U32)
        w2_sraw = tile("w2_sraw", [P, R], U8)
        late = tile("late", [P, R + 2 * N + O], U8)
        w1_sraw = late[:, 0:R]
        ws_s = late[:, R : R + N]
        wb_s = late[:, R + N : R + 2 * N]
        sx_s = late[:, R + 2 * N :]

        def w2_rows(q):
            four = w2_scales[0].bitcast(I32)[4 * q : 4 * q + 4, :]
            nc.sync.dma_start(
                out=w2_sraw[32 * q : 32 * (q + 1), :].bitcast(I32),
                in_=four.unsqueeze(0).broadcast_to([8, 4, R // 4]),
            )

        nc.vector.memset(xt_s[:].bitcast(I32), 0)
        nc.vector.memset(late[:].bitcast(I32), 0)
        nc.gpsimd.dma_start(out=w2_raw[:].bitcast(I32), in_=fp8_words(w2_words))
        nc.gpsimd.dma_start(out=w1_raw[:].bitcast(I32), in_=fp8_words(w_words))
        nc.sync.dma_start(out=list2[:], in_=offs2)
        w2_rows(0)
        nc.sync.dma_start(out=xt_w[:].bitcast(I32), in_=xt_words[0].bitcast(I32))
        load_scale_rows(nc.scalar, xt_s, xt_scales)
        warm_in = tile("warm_in", [P, 1], F32)
        warm_out = tile("warm_out", [P, 1], F32)
        nc.vector.memset(warm_in[:], 0.0)
        nc.scalar.activation(out=warm_out[:], in_=warm_in[:], func=ACT.Sigmoid)
        for q in range(1, QUADS):
            w2_rows(q)
        nc.sync.dma_start(out=list1[:], in_=offs)
        load_scale_rows(nc.sync, w1_sraw, w_scales)
        nc.sync.dma_start(out=list3[:], in_=offs3)
        nc.sync.dma_start(out=list4[:], in_=offs4)
        slope = tile("slope", [P, PACK], F32)
        nc.sync.dma_start(out=slope[:], in_=sg.rearrange("(p t) o -> p (t o)", t=PACK))

        halves = N // P
        gate_table = [tile("gate_table%d" % h, [P, E], F32) for h in range(halves)]
        gate_slope = tile("gate_slope", [P, halves], F32)
        gate_offset = tile("gate_offset", [P, halves], F32)
        ws_w = tile("ws_w", [P, N], U32)
        sx_w = tile("sx_w", [P, O], U32)
        wb_w = tile("wb_w", [P, 2 * N], U8)
        nc.gpsimd.dma_start(out=ws_w[:].bitcast(I32), in_=fp8_words(ws_words))
        nc.gpsimd.dma_start(out=sx_w[:].bitcast(I32), in_=fp8_words(sx_words))
        nc.gpsimd.dma_start(out=wb_w[:].bitcast(I32), in_=wb_words[0].bitcast(I32))
        nc.sync.dma_start(out=list5[:], in_=offs5)
        with nc.allow_non_contiguous_dma(reason="one value for each partition"):
            nc.sync.dma_start(out=gate_slope[:], in_=so.rearrange("(h p) o -> p (h o)", p=P))
            nc.sync.dma_start(out=gate_offset[:], in_=bo.rearrange("(h p) o -> p (h o)", p=P))
        load_scale_rows(nc.sync, ws_s, ws_scales)
        load_scale_rows(nc.sync, sx_s, sx_scales)
        load_scale_rows(nc.sync, wb_s, wb_scales)
        for h in range(halves):
            nc.sync.dma_start(out=gate_table[h][:], in_=tz[h * P : (h + 1) * P, :])

        def first_stage(name, offsets, raw, sraw, fmt, banks):
            picked_s = tile(name + "_picked_s", [P, J], U8)
            picked_w = tile(name + "_picked_w", [P, J], U16)
            dealt_w = tile(name + "_dealt_w", [P, R], U32)
            dealt_s = tile(name + "_dealt_s", [P, R], U8)
            nc.vector.tensor_copy(out=picked_s[:], in_=xt_s[:].indirect(offsets[:]))
            nc.vector.tensor_copy(out=picked_w[:], in_=xt_w[:].indirect(offsets[:]))
            nc.scalar.copy(
                out=dealt_w[:].rearrange("p (t m) -> p m t", t=PACK),
                in_=raw[:].rearrange("p (m t) -> p m t", t=PACK),
            )
            nc.vector.tensor_copy(
                out=dealt_s[:].rearrange("p (t m) -> p m t", t=PACK),
                in_=sraw.rearrange("p (m t) -> p m t", t=PACK),
            )
            for t in range(PACK):
                cols = slice(t * P, (t + 1) * P)
                nc.tensor.matmul_mx(
                    out=banks[t],
                    lhsT=dealt_w[:, cols].bitcast(fmt),
                    lhsT_scale=dealt_s[:, cols],
                    rhs=picked_w[:].bitcast(E2M1),
                    rhs_scale=picked_s[:],
                    start=True,
                    stop=True,
                )

        b_ps = [ps.tile([P, J], F32, name="b_ps%d" % t, tag="b_ps%d" % t) for t in range(PACK)]
        a_ps = [ps.tile([P, J], F32, name="a_ps%d" % t) for t in range(PACK)]
        first_stage("b", list2, w2_raw, w2_sraw[:], E5M2, [b_ps[t][:] for t in range(PACK)])
        b_sb = [tile("b_sb%d" % t, [P, J], F32) for t in range(PACK)]
        for t in range(PACK):
            nc.scalar.copy(out=b_sb[t][:], in_=b_ps[t][:])
        first_stage("a", list1, w1_raw, w1_sraw, E4M3, [a_ps[t][:] for t in range(PACK)])

        b3 = tile("b3", [P, PACK, O], F32)
        b4 = tile("b4", [P, PACK, O], F32)
        larger = tile("larger", [P, PACK, O], F32)
        gate = tile("gate", [P, PACK, O], F32)
        a_sb = [tile("a_sb%d" % t, [P, J], F32) for t in range(PACK)]
        for t in range(PACK):
            if t < 2:
                nc.scalar.activation(out=b3[:, t, :], in_=b_sb[t][:].indirect(list3[:]), func=ACT.Copy)
            else:
                nc.vector.tensor_copy(out=b3[:, t, :], in_=b_sb[t][:].indirect(list3[:]))
            nc.vector.tensor_copy(out=b4[:, t, :], in_=b_sb[t][:].indirect(list4[:]))
            if t == 1:
                nc.vector.tensor_copy(out=a_sb[t][:], in_=a_ps[t][:])
            else:
                nc.scalar.copy(out=a_sb[t][:], in_=a_ps[t][:])
            nc.scalar.activation(
                out=gate[:, t, :], in_=a_sb[t][:].indirect(list4[:]), func=ACT.Sigmoid, scale=slope[:, t : t + 1]
            )
        nc.vector.tensor_tensor(out=larger[:], in0=b3[:], in1=b4[:], op=ALU.max)
        hid = tile("hid", [P, O, PACK], BF16)
        nc.vector.tensor_tensor(
            out=hid[:].rearrange("p (c i) t -> p c t i", i=4),
            in0=larger[:].rearrange("p t (c i) -> p c t i", i=4),
            in1=gate[:].rearrange("p t (c i) -> p c t i", i=4),
            op=ALU.mult,
        )
        hid_w = tile("hid_w", [P, O], U32)
        hid_s = tile("hid_s", [P, O], U8)
        nc.vector.quantize_mx(
            out=hid_w[:].bitcast(E5M2), scales=hid_s[:], in_=hid[:].rearrange("p o t -> p (o t)")
        )

        stores = [nc.sync, nc.scalar]
        p_ps = [ps.tile([P, O], F32, name="p_ps%d" % h, tag="b_ps%d" % h) for h in range(halves)]
        for h in range(halves):
            cols = slice(h * P, (h + 1) * P)
            nc.tensor.matmul_mx(
                out=p_ps[h][:], lhsT=ws_w[:, cols].bitcast(E4M3), lhsT_scale=ws_s[:, cols],
                rhs=sx_w[:].bitcast(E4M3), rhs_scale=sx_s, start=True, stop=False,
            )
        for h in range(halves):
            cols = slice(h * P, (h + 1) * P)
            last_gate = tile("last_gate%d" % h, [P, O], F32)
            nc.scalar.activation(
                out=last_gate[:], in_=gate_table[h][:].indirect(list5[:]), func=ACT.Sigmoid,
                bias=gate_offset[:, h : h + 1], scale=gate_slope[:, h : h + 1],
            )
            nc.tensor.matmul_mx(
                out=p_ps[h][:], lhsT=wb_w[:, 2 * h * P : 2 * (h + 1) * P].bitcast(E2M1), lhsT_scale=wb_s[:, cols],
                rhs=hid_w[:].bitcast(E5M2), rhs_scale=hid_s[:], start=False, stop=True,
            )
            result = tile("result%d" % h, [P, O], F32)
            nc.vector.tensor_tensor(out=result[:], in0=p_ps[h][:], in1=last_gate[:], op=ALU.mult)
            stores[h].dma_start(out=out[cols, :], in_=result[:])
